import numpy as np
import ml_dtypes


def mxq(x, axis, fmt="e4m3"):
    dtype, down = {"e4m3": (ml_dtypes.float8_e4m3fn, 7), "e5m2": (ml_dtypes.float8_e5m2, 14)}[fmt]
    v = np.moveaxis(np.asarray(x, np.float32).astype(ml_dtypes.bfloat16).astype(np.float64), axis, -1)
    blocks = v.reshape(v.shape[:-1] + (-1, 32))
    amax = np.abs(blocks).max(-1, keepdims=True)
    byte = np.maximum(np.where(amax > 0, np.frexp(amax)[1] - 1 + 127, 0) - down, 1)
    scale = np.exp2(byte - 127.0)
    codes = (blocks / scale).astype(np.float32).astype(dtype).astype(np.float64)
    return np.moveaxis((codes * scale).reshape(v.shape), -1, axis)


WIDE = False


def mx_kscale(k):
    if not WIDE:
        return np.ones(k)
    levels = np.array([10, -10, 5, -5, 0])
    if k % 512:
        return np.exp2(np.random.permutation(np.resize(levels, k // 32))).repeat(32)
    a = np.empty((k // 512, 16))
    for p in range(k // 512):
        a[p, :8] = np.random.permutation(np.resize(levels, 8))
        for g in range(8):
            far = levels[np.abs(levels - a[p, g]) >= 10]
            a[p, g + 8] = far[np.random.randint(len(far))]
    return np.exp2(a.ravel()).repeat(32)


def f64(x):
    return np.asarray(x).astype(np.float64)


def striped(idx):
    return np.tile(idx.reshape(-1, 16).T, (8, 1)).astype(np.uint16)


def unstriped(offs):
    return offs[:16].T.reshape(-1).astype(np.int64)


E2M1 = np.array([0.0, 0.5, 1.0, 1.5, 2.0, 3.0, 4.0, 6.0, -0.0, -0.5, -1.0, -1.5, -2.0, -3.0, -4.0, -6.0])


def pack_weight(w, fmt):
    k, n = w.shape
    w = f64(np.asarray(w, np.float32).astype(ml_dtypes.bfloat16)).reshape(k // 32, 32, n)
    amax = np.abs(w).max(1)
    if fmt == "e4m3":
        byte = np.frexp(amax)[1] - 1 + 127 - 7
    else:
        mant, ex = np.frexp(amax / 6.0)
        byte = np.where(mant > 0.5, ex, ex - 1) + 127
    byte = np.clip(np.where(amax > 0, byte, 1), 1, 254)
    scaled = (w * np.exp2(127.0 - byte)[:, None, :]).reshape(k, n).astype(np.float32)
    by_word = np.ascontiguousarray(scaled.reshape(k // 512, 128, 4, n).transpose(0, 1, 3, 2))
    if fmt == "e4m3":
        words = by_word.astype(ml_dtypes.float8_e4m3fn).view(np.uint8)
    else:
        c = by_word.astype(ml_dtypes.float4_e2m1fn).view(np.uint8) & 0xF
        words = (c[..., 0::2] | (c[..., 1::2] << 4)).reshape(k // 512, 128, 2 * n)
    return np.ascontiguousarray(words), np.ascontiguousarray(byte.astype(np.uint8).reshape(k // 512, 16, n))


def unpack_weight(words, scales, fmt):
    g, _, n = scales.shape
    words = np.ascontiguousarray(words).reshape(g, 128, n, -1)
    if fmt == "e4m3":
        vals = words.view(ml_dtypes.float8_e4m3fn).astype(np.float64)
    else:
        nib = np.empty((g, 128, n, 4), np.uint8)
        nib[..., 0::2] = words & 0xF
        nib[..., 1::2] = words >> 4
        vals = E2M1[nib]
    vals = vals * np.repeat(np.exp2(scales.astype(np.float64) - 127.0), 8, axis=1)[..., None]
    return vals.transpose(0, 1, 3, 2).reshape(g * 512, n)


def gelu(v):
    return 0.5 * v * (1.0 + np.tanh(np.sqrt(2.0 / np.pi) * (v + 0.044715 * v**3)))


K, H, T, S, T2, S2, T3, P = 1024, 1024, 2048, 512, 1024, 512, 2048, 512


def setup_inputs():
    n = np.random.standard_normal
    s, u = mx_kscale(K)[:, None], mx_kscale(H)[:, None]
    tab_words, tab_scales = pack_weight(n((K, T)) * s, "e4m3")
    tab2_words, tab2_scales = pack_weight(n((H, T3)) / np.sqrt(H) / u, "e4m3")
    w1_words, w1_scales = pack_weight(1.5 * n((K, H)) / np.sqrt(K) / s, "e2m1")
    w3_words, w3_scales = pack_weight(n((K, H)) / np.sqrt(K) / s * u.T, "e4m3")
    return {
        "tab_words": tab_words, "tab_scales": tab_scales,
        "tab2_words": tab2_words, "tab2_scales": tab2_scales,
        "w1_words": w1_words, "w1_scales": w1_scales,
        "w2": (1.5 * n((K, H)) / np.sqrt(K) / s).astype(np.float32),
        "w3_words": w3_words, "w3_scales": w3_scales,
        "gain": (np.exp(0.3 * n(H)) * u[:, 0]).astype(np.float32),
        "wgs": np.exp(0.3 * n((128, S))).astype(np.float32),
        "page0": (n((H, T2)) * u).astype(np.float32),
        "closure": n((S2, P)).astype(np.float32),
        "offs": striped(np.random.permutation(T)[:S]),
        "offs2": striped(np.random.permutation(T3)[:S2]),
        "offs3": striped(np.random.permutation(T2)[:S]),
        "pos1": striped(np.random.permutation(T2)[:P]),
        "pos2": striped(np.random.permutation(T2)[:P]),
    }


def reference(tab_words, tab_scales, tab2_words, tab2_scales, w1_words, w1_scales, w2, w3_words, w3_scales,
              gain, wgs, page0, closure, offs, offs2, offs3, pos1, pos2):
    v = unpack_weight(tab_words, tab_scales, "e4m3")[:, unstriped(offs)]
    v2 = unpack_weight(tab2_words, tab2_scales, "e4m3")[:, unstriped(offs2)]
    a = unpack_weight(w1_words, w1_scales, "e2m1").T @ v
    b = mxq(f64(w2), 0, "e4m3").T @ v
    c = unpack_weight(w3_words, w3_scales, "e4m3").T @ v
    d = np.maximum(a, b)
    d = 0.5 * d * (1.0 + np.tanh(0.7978845608028654 * (d + 0.044715 * d * d * d)))
    h = f64(gain)[:, None] * d + c
    page = f64(page0).copy()
    page[:, unstriped(offs3)] = np.tile(f64(wgs), (H // 128, 1)) * h
    e = v2.T @ mxq(page, 0, "e4m3")
    return e[:, unstriped(pos1)] * e[:, unstriped(pos2)] + f64(closure)

@@ -1,0 +1,309 @@
+from contextlib import ExitStack
+
+import concourse.mybir as mybir
+
+K, H, T, S, T2 = 1024, 1024, 2048, 512, 1024
+FLOPS = 3 * 2 * K * H * S + 2 * H * S * T2
+
+F32 = mybir.dt.float32
+BF16 = mybir.dt.bfloat16
+I32 = mybir.dt.int32
+U32 = mybir.dt.uint32
+U16 = mybir.dt.uint16
+U8 = mybir.dt.uint8
+FP8X4 = mybir.dt.float8_e4m3fn_x4
+FP4X4 = mybir.dt.float4_e2m1fn_x4
+ALU = mybir.AluOpType
+ACT = mybir.ActivationFunctionType
+
+P = 128
+PACK = 4
+KP = 512
+N = 512
+VECTOR_COLS = 640
+
+
+def tile_list_passage_tie_scores_kernel(tc, tab_words, tab_scales, tab2_words, tab2_scales, w1_words, w1_scales,
+                                                  w2, w3_words, w3_scales, gain, wgs, page0, closure,
+                                                  offs, offs2, offs3, pos1, pos2, out):
+    nc = tc.nc
+    with ExitStack() as ctx:
+        keep = ctx.enter_context(tc.tile_pool(name="keep", bufs=1))
+        two = ctx.enter_context(tc.tile_pool(name="two", bufs=2))
+        four = ctx.enter_context(tc.tile_pool(name="four", bufs=4))
+        psum = ctx.enter_context(tc.psum_pool(name="psum", bufs=2))
+
+        def load_list(src, name):
+            t = keep.tile([P, S // 16], U16, name=name)
+            nc.sync.dma_start(t[:], src)
+            return t
+
+        def load_words(src, pool, name, tag):
+            t = pool.tile([P, T], U32, name=name, tag=tag, align_bytes=64)
+            nc.sync.dma_start(t[:].bitcast(I32), src.rearrange("p n t -> p (n t)").bitcast(I32))
+            return t
+
+        def load_w2(a, b):
+            t = four.tile([P, PACK, KP], F32, name="w2raw", tag="raw", align_bytes=64)
+            nc.sync.dma_start(t[:], w2[a * KP:(a + 1) * KP, b * KP:(b + 1) * KP].rearrange("(p j) c -> p j c", j=PACK))
+            return t
+
+        def load_w3(b):
+            t = keep.tile([P, 2, KP], I32, name="w3raw%d" % b, align_bytes=64)
+            src = w3_words.rearrange("a p n t -> p a (n t)")[:, :, b * KP * 4:(b + 1) * KP * 4].bitcast(I32)
+            nc.sync.dma_start(t[:], src)
+            return t
+
+        def load_w1(b):
+            t = keep.tile([P, 2, 2 * KP], U8, name="w1raw%d" % b, align_bytes=64)
+            src = w1_words.rearrange("a p n -> p a n")[:, :, b * KP * 2:(b + 1) * KP * 2].bitcast(I32)
+            nc.sync.dma_start(t[:].bitcast(I32), src)
+            return t
+
+        page_rows = page0.rearrange("(b p t) n -> b t p n", b=2, t=PACK)
+
+        def load_page(i):
+            t = keep.tile([P, T2], F32, name="page%d" % i, align_bytes=64)
+            nc.sync.dma_start(t[:], page_rows[i // PACK, i % PACK])
+            return t
+
+        tabs = keep.tile([P, 2 * T], U8, name="tabs", align_bytes=64)
+        w1sraw = keep.tile([P, 2 * H], U8, name="w1sraw", align_bytes=64)
+        w3sraw = keep.tile([P, H], U8, name="w3sraw", align_bytes=64)
+        tab2s = keep.tile([P, T], U8, name="tab2s", align_bytes=64)
+        nc.vector.memset(tabs[:].bitcast(I32), 0)
+        nc.gpsimd.memset(w1sraw[:].bitcast(I32), 0)
+        nc.gpsimd.memset(w3sraw[:].bitcast(I32), 0)
+        nc.gpsimd.memset(tab2s[:].bitcast(I32), 0)
+
+        def load_scales_beside(dst, src):
+            for q in range(4):
+                nc.sync.dma_start(dst[32 * q:32 * q + 4, :].bitcast(I32).rearrange("r (a n) -> r a n", a=2),
+                                  src.bitcast(I32)[:, 4 * q:4 * q + 4, :].rearrange("a r n -> r a n"))
+
+        def load_scales_below(dst, src):
+            for q in range(4):
+                nc.sync.dma_start(dst[32 * q:32 * q + 8, :].bitcast(I32), src.bitcast(I32)[:, 4 * q:4 * q + 4, :])
+
+        def load_wgs(lo, hi):
+            t = keep.tile([P, (hi - lo) * S], F32, name="wgs%d" % lo, align_bytes=64)
+            for q in (0, 2, 1, 3):
+                nc.sync.dma_start(t[32 * q:32 * q + 32, :], wgs.rearrange("(r t) s -> r (t s)", t=PACK)[:, lo * S:hi * S])
+            return [t[:, j * S:(j + 1) * S] for j in range(hi - lo)]
+
+        tabw = [None, None]
+        w2raw = {}
+        tabw[0] = load_words(tab_words[0], two, "tabw", "eightk")
+        load_scales_beside(tabs, tab_scales)
+        l_offs = load_list(offs, "l_offs")
+        w1raw = [load_w1(0), None]
+        w2raw[0, 0] = load_w2(0, 0)
+        load_scales_beside(w1sraw, w1_scales)
+        tabw[1] = load_words(tab_words[1], two, "tabw", "eightk")
+        w2raw[1, 0] = load_w2(1, 0)
+        load_scales_below(w3sraw, w3_scales)
+        w3raw = [load_w3(0), None]
+        w1raw[1] = load_w1(1)
+        gain_sb = keep.tile([P, 2, PACK], F32, name="gain_sb")
+        nc.sync.dma_start(gain_sb[:], gain.rearrange("(b p t) -> p b t", b=2, t=PACK))
+        l_offs3 = load_list(offs3, "l_offs3")
+        page = [load_page(0)]
+        wgs_sb = load_wgs(0, 1)
+        w2raw[0, 1] = load_w2(0, 1)
+        wgs_sb.extend(load_wgs(1, PACK))
+        page.append(load_page(1))
+        w2raw[1, 1] = load_w2(1, 1)
+        w3raw[1] = load_w3(1)
+        page.extend([load_page(i) for i in range(2, 8)])
+        l_offs2 = load_list(offs2, "l_offs2")
+        tab2w = [load_words(tab2_words[a], keep, "tab2w%d" % a, "tab2w%d" % a) for a in range(2)]
+        load_scales_below(tab2s, tab2_scales)
+        l_pos1 = load_list(pos1, "l_pos1")
+        l_pos2 = load_list(pos2, "l_pos2")
+
+        vw = keep.tile([P, 2, S], U32, name="vw", align_bytes=64)
+        vs = keep.tile([P, 2, S], U8, name="vs", align_bytes=64)
+        w1p = [keep.tile([P, 2, 2 * KP], U8, name="w1p%d" % b, align_bytes=64) for b in range(2)]
+        w1sp = keep.tile([P, 2 * H], U8, name="w1sp", align_bytes=64)
+        w3sp = keep.tile([P, H], U8, name="w3sp", align_bytes=64)
+        w3p = [None, None]
+        w2c = {}
+        w2s = {}
+
+        def gather_words(a):
+            nc.vector.tensor_copy(vw[:, a, :], tabw[a][:].indirect(l_offs[:]))
+
+        def gather_scales(a):
+            nc.vector.tensor_copy(vs[:, a, :], tabs[:, a * T:(a + 1) * T].indirect(l_offs[:]))
+
+        def round_w2(a, b, tag, split):
+            g = keep.tile([P, PACK, P, PACK], BF16, name="w2bf", tag=tag, align_bytes=64)
+            dst = g[:].rearrange("p t m j -> p m j t")
+            src = w2raw[a, b][:].rearrange("p j (m t) -> p m j t", t=PACK)
+            if split < P:
+                nc.scalar.copy(dst[:, split:], src[:, split:])
+            if split:
+                nc.vector.tensor_copy(dst[:, :split], src[:, :split])
+            return g
+
+        def quantize_w2(a, b, g, cuts, tag):
+            w2c[a, b] = keep.tile([P, KP], U32, name="w2c", tag=tag, align_bytes=64)
+            w2s[a, b] = keep.tile([P, KP], U8, name="w2s%d%d" % (a, b), align_bytes=64)
+            flat = g[:].rearrange("p t m j -> p (t m j)")
+            for lo, hi in cuts:
+                nc.vector.quantize_mx(out=w2c[a, b][:, lo:hi].bitcast(FP8X4), scales=w2s[a, b][:, lo:hi],
+                                      in_=flat[:, PACK * lo:PACK * hi])
+
+        def deal_scales(dst, src):
+            nc.vector.tensor_copy(dst[:].rearrange("p (g t m) -> p g t m", t=PACK, m=P),
+                                  src[:].rearrange("p (g m t) -> p g t m", t=PACK, m=P))
+
+        def deal_w1(b):
+            nc.vector.tensor_copy(w1p[b][:].bitcast(U16).rearrange("p a (t m) -> p a t m", t=PACK),
+                                  w1raw[b][:].bitcast(U16).rearrange("p a (m t) -> p a t m", t=PACK))
+
+        def deal_w3(b, tag):
+            w3p[b] = keep.tile([P, 2, KP], U32, name="w3p", tag=tag, align_bytes=64)
+            nc.vector.tensor_copy(w3p[b][:].bitcast(I32).rearrange("p a (t m) -> p a m t", t=PACK),
+                                  w3raw[b][:].rearrange("p a (m t) -> p a m t", t=PACK))
+
+        gather_words(0)
+        gather_scales(0)
+        gather_scales(1)
+        deal_w1(0)
+        deal_scales(w1sp, w1sraw)
+        g00 = round_w2(0, 0, "wov0", 0)
+        gather_words(1)
+        quantize_w2(0, 0, g00, [(0, KP)], "w2c00")
+        g10 = round_w2(1, 0, "wov1", P)
+        quantize_w2(1, 0, g10, [(0, P), (P, KP)], "w2c10")
+        deal_scales(w3sp, w3sraw)
+        deal_w3(0, "w3p0")
+
+        def product(tag, i, lhs, lhs_scale):
+            acc = psum.tile([P, N], F32, name=tag, tag=tag)
+            for a in range(2):
+                nc.tensor.matmul_mx(out=acc[:], lhsT=lhs(a), lhsT_scale=lhs_scale(a), rhs=vw[:, a, :].bitcast(FP8X4),
+                                    rhs_scale=vs[:, a, :], start=(a == 0), stop=(a == 1))
+            return acc
+
+        def gated(i):
+            b, t = divmod(i, PACK)
+            tags = ("pa", "pb") if i // 2 % 2 == 0 else ("pb", "pa")
+            pa = product(tags[0], i, lambda a: w1p[b][:, a, 2 * t * P:2 * (t + 1) * P].bitcast(FP4X4),
+                         lambda a: w1sp[:, a * H + i * P:a * H + (i + 1) * P])
+            pb = product(tags[1], i, lambda a: w2c[a, b][:, t * P:(t + 1) * P].bitcast(FP8X4),
+                         lambda a: w2s[a, b][:, t * P:(t + 1) * P])
+            x = keep.tile([P, N], F32, name="x", tag="x%d" % i, align_bytes=64)
+            xa = keep.tile([P, N], F32, name="xa", tag="h3", align_bytes=64) if i == 4 else x
+            nc.scalar.copy(xa[:], pa[:])
+            nc.vector.tensor_tensor(x[:], xa[:], pb[:], ALU.max)
+            g = two.tile([P, N], F32, name="g", tag="g", align_bytes=64)
+            nc.scalar.activation(g[:], x[:], ACT.Gelu_apprx_tanh)
+            return g
+
+        def linear(i):
+            b, t = divmod(i, PACK)
+            return product("pc", i, lambda a: w3p[b][:, a, t * P:(t + 1) * P].bitcast(FP8X4),
+                           lambda a: w3sp[4 * a:P, i * P:(i + 1) * P])
+
+        def put(i, g, pc):
+            b, t = divmod(i, PACK)
+            h = keep.tile([P, N], F32, name="h", tag={1: "x1", 2: "x2"}.get(i, "h%d" % i), align_bytes=64)
+            nc.vector.scalar_tensor_tensor(h[:], g[:], gain_sb[:, b, t:t + 1], pc[:], ALU.mult, ALU.add)
+            nc.vector.tensor_tensor(page[i][:].indirect(l_offs3[:]), h[:], wgs_sb[t], ALU.mult)
+
+        pcodes = [keep.tile([P, T2], U32, name="pcodes%d" % b, align_bytes=64) for b in range(2)]
+        pscales = [keep.tile([P, T2], U8, name="pscales%d" % b, align_bytes=64) for b in range(2)]
+
+        def weave(copy, dst, planes, lo, hi):
+            copy(dst.rearrange("p (c i) t -> p c t i", i=4), planes[:, :, lo:hi].rearrange("p t (c i) -> p c t i", i=4))
+
+        def quantize_page(b, lo, hi, woven):
+            nc.vector.quantize_mx(out=pcodes[b][:, lo:hi].bitcast(FP8X4), scales=pscales[b][:, lo:hi],
+                                  in_=woven[:].rearrange("p n t -> p (n t)"))
+
+        planes = [keep.tile([P, PACK, T2], BF16, name="planes0", align_bytes=64), None]
+
+        v2w = {}
+        v2s = {}
+
+        def gather_v2(part):
+            entries = l_offs2[:, part * 16:(part + 1) * 16]
+            for a in range(2):
+                v2w[part, a] = keep.tile([P, S // 2], U32, name="v2w", tag=(("h4", "h5"), ("wov0", "wov1"))[part][a], align_bytes=64)
+                nc.vector.tensor_copy(v2w[part, a][:], tab2w[a][:].indirect(entries))
+            v2s[part] = keep.tile([P, S // 2], U8, name="v2s", tag=("page4", "page7")[part], align_bytes=64)
+            nc.vector.tensor_copy(v2s[part][:], tab2s[:].indirect(entries))
+
+        g_next = gated(0)
+        pc_next = linear(0)
+        deal_w1(1)
+        for i in range(8):
+            b, t = divmod(i, PACK)
+            g_now, pc_now = g_next, pc_next
+            if i + 1 < 8:
+                g_next = gated(i + 1)
+            if i == 1:
+                quantize_w2(0, 1, round_w2(0, 1, "x1", 0), [(0, KP)], "h0")
+            if i == 2:
+                quantize_w2(1, 1, round_w2(1, 1, "x2", 0), [(0, KP)], "x1")
+                deal_w3(1, "page1")
+            if i + 1 < 8:
+                pc_next = linear(i + 1)
+            put(i, g_now, pc_now)
+            if i == 4:
+                planes[1] = two.tile([P, PACK, T2], BF16, name="planes1", tag="eightk", align_bytes=64)
+            if i < 7:
+                nc.scalar.copy(planes[b][:, t, :], page[i][:])
+            if 3 <= i < 7:
+                lo = (i - 3) * 256
+                woven = keep.tile([P, 256, PACK], BF16, name="woven", tag="x%d" % (i + 1), align_bytes=64)
+                weave(nc.scalar.copy, woven[:], planes[0], lo, lo + 256)
+                quantize_page(0, lo, lo + 256, woven)
+            if i == 5:
+                gather_v2(0)
+
+        clo = two.tile([P, 4, N], F32, name="clo", tag="eightk", align_bytes=64)
+        nc.sync.dma_start(clo[:], closure.rearrange("(u p) j -> p u j", p=P))
+
+        banks = [[psum.tile([P, N], F32, name=tag, tag=tag) for half in range(2)] for tag in ("pe", "pa", "pb", "pc")]
+
+        def score(u, half, b):
+            cols = slice(half * N, (half + 1) * N)
+            nc.tensor.matmul_mx(out=banks[u][half][:], lhsT=v2w[u // 2, b][:, u % 2 * P:(u % 2 + 1) * P].bitcast(FP8X4),
+                                lhsT_scale=v2s[u // 2][4 * b:P, u % 2 * P:(u % 2 + 1) * P], rhs=pcodes[b][:, cols].bitcast(FP8X4),
+                                rhs_scale=pscales[b][:, cols], start=(b == 0), stop=(b == 1))
+
+        for u in range(2):
+            for half in range(2):
+                score(u, half, 0)
+
+        nc.vector.tensor_copy(planes[1][:, 3, :], page[7][:])
+        wov = [keep.tile([P, N, PACK], BF16, name="wov", tag="wov%d" % half, align_bytes=64) for half in range(2)]
+        weave(nc.scalar.copy, wov[1][:, VECTOR_COLS - N:, :], planes[1], VECTOR_COLS, T2)
+        weave(nc.vector.tensor_copy, wov[0][:], planes[1], 0, N)
+        weave(nc.vector.tensor_copy, wov[1][:, :VECTOR_COLS - N, :], planes[1], N, VECTOR_COLS)
+        for half in range(2):
+            quantize_page(1, half * N, (half + 1) * N, wov[half])
+
+        gather_v2(1)
+        for u in range(4):
+            for half in range(2):
+                if u >= 2:
+                    score(u, half, 0)
+                score(u, half, 1)
+            e = four.tile([P, T2], F32, name="e", tag="raw", align_bytes=64)
+            if u == 0:
+                nc.scalar.copy(e[:, :N], banks[u][0][:])
+                nc.vector.tensor_copy(e[:, N:], banks[u][1][:])
+            else:
+                for half in range(2):
+                    nc.scalar.copy(e[:, half * N:(half + 1) * N], banks[u][half][:])
+            first = keep.tile([P, N], F32, name="first", tag="x%d" % (4 + u), align_bytes=64)
+            nc.vector.tensor_copy(first[:], e[:].indirect(l_pos1[:]))
+            prod = two.tile([P, N], F32, name="prod", tag="g", align_bytes=64)
+            nc.vector.tensor_tensor(prod[:], e[:].indirect(l_pos2[:]), first[:], ALU.mult)
+            res = keep.tile([P, N], F32, name="res", tag="h%d" % (6 + u % 2), align_bytes=64)
+            nc.vector.tensor_tensor(res[:], prod[:], clo[:, u, :], ALU.add)
+            nc.sync.dma_start(out[u * P:(u + 1) * P, :], res[:])

@@ -1,6 +1,7 @@
 from contextlib import ExitStack
 
 import concourse.mybir as mybir
+from concourse.masks import make_identity
 
 K, H, T, S, T2 = 1024, 1024, 2048, 512, 1024
 FLOPS = 3 * 2 * K * H * S + 2 * H * S * T2
@@ -30,7 +31,6 @@ def tile_list_passage_tie_scores_kernel(tc, tab_words, tab_scales, tab2_words, t
     with ExitStack() as ctx:
         keep = ctx.enter_context(tc.tile_pool(name="keep", bufs=1))
         two = ctx.enter_context(tc.tile_pool(name="two", bufs=2))
-        four = ctx.enter_context(tc.tile_pool(name="four", bufs=4))
         psum = ctx.enter_context(tc.psum_pool(name="psum", bufs=2))
 
         def load_list(src, name):
@@ -44,7 +44,7 @@ def tile_list_passage_tie_scores_kernel(tc, tab_words, tab_scales, tab2_words, t
             return t
 
         def load_w2(a, b):
-            t = four.tile([P, PACK, KP], F32, name="w2raw", tag="raw", align_bytes=64)
+            t = keep.tile([P, PACK, KP], F32, name="w2raw", tag="raw%d%d" % (a, b), align_bytes=64)
             nc.sync.dma_start(t[:], w2[a * KP:(a + 1) * KP, b * KP:(b + 1) * KP].rearrange("(p j) c -> p j c", j=PACK))
             return t
 
@@ -72,9 +72,14 @@ def tile_list_passage_tie_scores_kernel(tc, tab_words, tab_scales, tab2_words, t
         w3sraw = keep.tile([P, H], U8, name="w3sraw", align_bytes=64)
         tab2s = keep.tile([P, T], U8, name="tab2s", align_bytes=64)
         nc.vector.memset(tabs[:].bitcast(I32), 0)
+        warm = keep.tile([P, 2], F32, name="warm")
+        nc.gpsimd.memset(warm[:, 0:1], 0.0)
+        nc.scalar.activation(warm[:, 1:2], warm[:, 0:1], ACT.Gelu_apprx_tanh)
         nc.gpsimd.memset(w1sraw[:].bitcast(I32), 0)
         nc.gpsimd.memset(w3sraw[:].bitcast(I32), 0)
         nc.gpsimd.memset(tab2s[:].bitcast(I32), 0)
+        ident = keep.tile([P, P], F32, name="ident", align_bytes=64)
+        make_identity(nc, ident[:])
 
         def load_scales_beside(dst, src):
             for q in range(4):
@@ -85,39 +90,34 @@ def tile_list_passage_tie_scores_kernel(tc, tab_words, tab_scales, tab2_words, t
             for q in range(4):
                 nc.sync.dma_start(dst[32 * q:32 * q + 8, :].bitcast(I32), src.bitcast(I32)[:, 4 * q:4 * q + 4, :])
 
-        def load_wgs(lo, hi):
-            t = keep.tile([P, (hi - lo) * S], F32, name="wgs%d" % lo, align_bytes=64)
-            for q in (0, 2, 1, 3):
-                nc.sync.dma_start(t[32 * q:32 * q + 32, :], wgs.rearrange("(r t) s -> r (t s)", t=PACK)[:, lo * S:hi * S])
-            return [t[:, j * S:(j + 1) * S] for j in range(hi - lo)]
-
         tabw = [None, None]
         w2raw = {}
         tabw[0] = load_words(tab_words[0], two, "tabw", "eightk")
         load_scales_beside(tabs, tab_scales)
         l_offs = load_list(offs, "l_offs")
-        w1raw = [load_w1(0), None]
+        wgs_raw = keep.tile([P, S], F32, name="wgs_raw", align_bytes=64)
+        nc.sync.dma_start(wgs_raw[:], wgs)
         w2raw[0, 0] = load_w2(0, 0)
         load_scales_beside(w1sraw, w1_scales)
+        w1raw = [load_w1(0), None]
         tabw[1] = load_words(tab_words[1], two, "tabw", "eightk")
-        w2raw[1, 0] = load_w2(1, 0)
         load_scales_below(w3sraw, w3_scales)
+        w2raw[1, 0] = load_w2(1, 0)
         w3raw = [load_w3(0), None]
-        w1raw[1] = load_w1(1)
         gain_sb = keep.tile([P, 2, PACK], F32, name="gain_sb")
         nc.sync.dma_start(gain_sb[:], gain.rearrange("(b p t) -> p b t", b=2, t=PACK))
         l_offs3 = load_list(offs3, "l_offs3")
         page = [load_page(0)]
-        wgs_sb = load_wgs(0, 1)
+        w1raw[1] = load_w1(1)
         w2raw[0, 1] = load_w2(0, 1)
-        wgs_sb.extend(load_wgs(1, PACK))
         page.append(load_page(1))
         w2raw[1, 1] = load_w2(1, 1)
         w3raw[1] = load_w3(1)
-        page.extend([load_page(i) for i in range(2, 8)])
+        page.extend([load_page(i) for i in range(2, 4)])
         l_offs2 = load_list(offs2, "l_offs2")
         tab2w = [load_words(tab2_words[a], keep, "tab2w%d" % a, "tab2w%d" % a) for a in range(2)]
         load_scales_below(tab2s, tab2_scales)
+        page.extend([load_page(i) for i in range(4, 8)])
         l_pos1 = load_list(pos1, "l_pos1")
         l_pos2 = load_list(pos2, "l_pos2")
 
@@ -136,14 +136,11 @@ def tile_list_passage_tie_scores_kernel(tc, tab_words, tab_scales, tab2_words, t
         def gather_scales(a):
             nc.vector.tensor_copy(vs[:, a, :], tabs[:, a * T:(a + 1) * T].indirect(l_offs[:]))
 
-        def round_w2(a, b, tag, split):
+        def round_w2(a, b, tag):
             g = keep.tile([P, PACK, P, PACK], BF16, name="w2bf", tag=tag, align_bytes=64)
             dst = g[:].rearrange("p t m j -> p m j t")
             src = w2raw[a, b][:].rearrange("p j (m t) -> p m j t", t=PACK)
-            if split < P:
-                nc.scalar.copy(dst[:, split:], src[:, split:])
-            if split:
-                nc.vector.tensor_copy(dst[:, :split], src[:, :split])
+            nc.scalar.copy(dst, src)
             return g
 
         def quantize_w2(a, b, g, cuts, tag):
@@ -172,13 +169,13 @@ def tile_list_passage_tie_scores_kernel(tc, tab_words, tab_scales, tab2_words, t
         gather_scales(1)
         deal_w1(0)
         deal_scales(w1sp, w1sraw)
-        g00 = round_w2(0, 0, "wov0", 0)
+        g00 = round_w2(0, 0, "wov0")
         gather_words(1)
         quantize_w2(0, 0, g00, [(0, KP)], "w2c00")
-        g10 = round_w2(1, 0, "wov1", P)
-        quantize_w2(1, 0, g10, [(0, P), (P, KP)], "w2c10")
         deal_scales(w3sp, w3sraw)
+        g10 = round_w2(1, 0, "x1")
         deal_w3(0, "w3p0")
+        quantize_w2(1, 0, g10, [(0, P), (P, KP)], "w3raw0")
 
         def product(tag, i, lhs, lhs_scale):
             acc = psum.tile([P, N], F32, name=tag, tag=tag)
@@ -187,6 +184,8 @@ def tile_list_passage_tie_scores_kernel(tc, tab_words, tab_scales, tab2_words, t
                                     rhs_scale=vs[:, a, :], start=(a == 0), stop=(a == 1))
             return acc
 
+        max_tag = {4: "x4", 5: "x5", 6: "h3", 7: "h4"}
+
         def gated(i):
             b, t = divmod(i, PACK)
             tags = ("pa", "pb") if i // 2 % 2 == 0 else ("pb", "pa")
@@ -194,8 +193,8 @@ def tile_list_passage_tie_scores_kernel(tc, tab_words, tab_scales, tab2_words, t
                          lambda a: w1sp[:, a * H + i * P:a * H + (i + 1) * P])
             pb = product(tags[1], i, lambda a: w2c[a, b][:, t * P:(t + 1) * P].bitcast(FP8X4),
                          lambda a: w2s[a, b][:, t * P:(t + 1) * P])
-            x = keep.tile([P, N], F32, name="x", tag="x%d" % i, align_bytes=64)
-            xa = keep.tile([P, N], F32, name="xa", tag="h3", align_bytes=64) if i == 4 else x
+            xa = keep.tile([P, N], F32, name="xa", tag={0: "raw10", 4: "h3"}.get(i, "x%d" % i), align_bytes=64)
+            x = keep.tile([P, N], F32, name="x", tag=max_tag[i], align_bytes=64) if i in (4, 6, 7) else xa
             nc.scalar.copy(xa[:], pa[:])
             nc.vector.tensor_tensor(x[:], xa[:], pb[:], ALU.max)
             g = two.tile([P, N], F32, name="g", tag="g", align_bytes=64)
@@ -207,11 +206,14 @@ def tile_list_passage_tie_scores_kernel(tc, tab_words, tab_scales, tab2_words, t
             return product("pc", i, lambda a: w3p[b][:, a, t * P:(t + 1) * P].bitcast(FP8X4),
                            lambda a: w3sp[4 * a:P, i * P:(i + 1) * P])
 
-        def put(i, g, pc):
+        def combine(i, g, pc):
             b, t = divmod(i, PACK)
             h = keep.tile([P, N], F32, name="h", tag={1: "x1", 2: "x2"}.get(i, "h%d" % i), align_bytes=64)
             nc.vector.scalar_tensor_tensor(h[:], g[:], gain_sb[:, b, t:t + 1], pc[:], ALU.mult, ALU.add)
-            nc.vector.tensor_tensor(page[i][:].indirect(l_offs3[:]), h[:], wgs_sb[t], ALU.mult)
+            return h
+
+        def put(i, h):
+            nc.vector.tensor_tensor(page[i][:].indirect(l_offs3[:]), h[:], wgs_sb[i % PACK], ALU.mult)
 
         pcodes = [keep.tile([P, T2], U32, name="pcodes%d" % b, align_bytes=64) for b in range(2)]
         pscales = [keep.tile([P, T2], U8, name="pscales%d" % b, align_bytes=64) for b in range(2)]
@@ -223,51 +225,84 @@ def tile_list_passage_tie_scores_kernel(tc, tab_words, tab_scales, tab2_words, t
             nc.vector.quantize_mx(out=pcodes[b][:, lo:hi].bitcast(FP8X4), scales=pscales[b][:, lo:hi],
                                   in_=woven[:].rearrange("p n t -> p (n t)"))
 
-        planes = [keep.tile([P, PACK, T2], BF16, name="planes0", align_bytes=64), None]
+        planes = [None, None]
 
         v2w = {}
         v2s = {}
 
-        def gather_v2(part):
-            entries = l_offs2[:, part * 16:(part + 1) * 16]
-            for a in range(2):
-                v2w[part, a] = keep.tile([P, S // 2], U32, name="v2w", tag=(("h4", "h5"), ("wov0", "wov1"))[part][a], align_bytes=64)
-                nc.vector.tensor_copy(v2w[part, a][:], tab2w[a][:].indirect(entries))
-            v2s[part] = keep.tile([P, S // 2], U8, name="v2s", tag=("page4", "page7")[part], align_bytes=64)
-            nc.vector.tensor_copy(v2s[part][:], tab2s[:].indirect(entries))
+        def gather_v2_words(part, a, tag):
+            v2w[part, a] = keep.tile([P, S // 2], U32, name="v2w", tag=tag, align_bytes=64)
+            nc.vector.tensor_copy(v2w[part, a][:], tab2w[a][:].indirect(l_offs2[:, part * 16:(part + 1) * 16]))
 
-        g_next = gated(0)
-        pc_next = linear(0)
+        def gather_v2_scales(part, tag):
+            v2s[part] = keep.tile([P, S // 2], U8, name="v2s", tag=tag, align_bytes=64)
+            nc.vector.tensor_copy(v2s[part][:], tab2s[:].indirect(l_offs2[:, part * 16:(part + 1) * 16]))
+
+        def weave_rows(copy, half, lo, hi):
+            copy(wov[half][:, :, lo:hi], planes[1][:, lo:hi, half * N:(half + 1) * N].rearrange("p t n -> p n t"))
+
+        def turn(dst, src):
+            for k in range(4):
+                nc.tensor.transpose(dst[:, k * P:(k + 1) * P], src[:, k * P:(k + 1) * P], ident[:])
+
+        def spread_wgs(t):
+            rep = keep.tile([P, 4, 4, 32], F32, name="rep", tag="rep" if t < 3 else "page0", align_bytes=64)
+            rows = wgs_t[:].rearrange("p (k q t) -> p k q t", k=4, t=PACK)[:, :, :, t]
+            nc.scalar.copy(rep[:], rows.unsqueeze(2).to_broadcast([P, 4, 4, 32]))
+            back = psum.tile([P, N], F32, name="back", tag="back", bufs=1)
+            turn(back, rep[:].rearrange("p k c q -> p (k c q)"))
+            dealt = keep.tile([P, S], F32, name="wgs%d" % t, align_bytes=64)
+            nc.scalar.copy(dealt[:], back[:])
+            return dealt[:]
+
+        wgs_t = psum.tile([P, N], F32, name="wgs_t", tag="fore", bufs=1)
+        turn(wgs_t, wgs_raw)
+        wgs_sb = [spread_wgs(t) for t in range(3)]
+        gs = [gated(0)]
+        pcs = [linear(0)]
+        gs.append(gated(1))
+        pcs.append(linear(1))
         deal_w1(1)
+        wov = [keep.tile([P, N, PACK], BF16, name="wov", tag="wov%d" % half, align_bytes=64) for half in range(2)]
         for i in range(8):
             b, t = divmod(i, PACK)
-            g_now, pc_now = g_next, pc_next
-            if i + 1 < 8:
-                g_next = gated(i + 1)
             if i == 1:
-                quantize_w2(0, 1, round_w2(0, 1, "x1", 0), [(0, KP)], "h0")
+                quantize_w2(0, 1, round_w2(0, 1, "x1"), [(0, KP)], "h0")
             if i == 2:
-                quantize_w2(1, 1, round_w2(1, 1, "x2", 0), [(0, KP)], "x1")
+                quantize_w2(1, 1, round_w2(1, 1, "x2"), [(0, KP)], "x1")
+                planes[0] = keep.tile([P, PACK, T2], BF16, name="planes0", tag="raw11", align_bytes=64)
+                nc.scalar.copy(planes[0][:, 0, :], page[0][:])
+                wgs_sb.append(spread_wgs(3))
+                nc.scalar.copy(planes[0][:, 1, :], page[1][:])
+            h = combine(i, gs[i], pcs[i])
+            if i == 2:
                 deal_w3(1, "page1")
-            if i + 1 < 8:
-                pc_next = linear(i + 1)
-            put(i, g_now, pc_now)
+            if i + 2 < 8:
+                gs.append(gated(i + 2))
+                pcs.append(linear(i + 2))
+            else:
+                gather_v2_words(0, i - 6, "h%d" % (i - 1))
+            put(i, h)
             if i == 4:
                 planes[1] = two.tile([P, PACK, T2], BF16, name="planes1", tag="eightk", align_bytes=64)
-            if i < 7:
+            if 2 <= i < 7:
                 nc.scalar.copy(planes[b][:, t, :], page[i][:])
             if 3 <= i < 7:
                 lo = (i - 3) * 256
-                woven = keep.tile([P, 256, PACK], BF16, name="woven", tag="x%d" % (i + 1), align_bytes=64)
+                woven = keep.tile([P, 256, PACK], BF16, name="woven", tag=max_tag[i + 1], align_bytes=64)
                 weave(nc.scalar.copy, woven[:], planes[0], lo, lo + 256)
                 quantize_page(0, lo, lo + 256, woven)
             if i == 5:
-                gather_v2(0)
+                gather_v2_scales(0, "page4")
+                weave_rows(nc.scalar.copy, 0, 0, 2)
+            if i == 6:
+                weave_rows(nc.scalar.copy, 1, 0, 3)
 
         clo = two.tile([P, 4, N], F32, name="clo", tag="eightk", align_bytes=64)
         nc.sync.dma_start(clo[:], closure.rearrange("(u p) j -> p u j", p=P))
 
-        banks = [[psum.tile([P, N], F32, name=tag, tag=tag) for half in range(2)] for tag in ("pe", "pa", "pb", "pc")]
+        banks = [[psum.tile([P, N], F32, name="bank", tag=tag, bufs=1) for tag in ("fore", "back")]]
+        banks.extend([[psum.tile([P, N], F32, name="bank", tag=tag) for half in range(2)] for tag in ("pa", "pb", "pc")])
 
         def score(u, half, b):
             cols = slice(half * N, (half + 1) * N)
@@ -279,31 +314,40 @@ def tile_list_passage_tie_scores_kernel(tc, tab_words, tab_scales, tab2_words, t
             for half in range(2):
                 score(u, half, 0)
 
-        nc.vector.tensor_copy(planes[1][:, 3, :], page[7][:])
-        wov = [keep.tile([P, N, PACK], BF16, name="wov", tag="wov%d" % half, align_bytes=64) for half in range(2)]
-        weave(nc.scalar.copy, wov[1][:, VECTOR_COLS - N:, :], planes[1], VECTOR_COLS, T2)
-        weave(nc.vector.tensor_copy, wov[0][:], planes[1], 0, N)
-        weave(nc.vector.tensor_copy, wov[1][:, :VECTOR_COLS - N, :], planes[1], N, VECTOR_COLS)
+        nc.scalar.copy(wov[1][:, :, 3], page[7][:, N:])
+        nc.vector.tensor_copy(planes[1][:, 3, :N], page[7][:, :N])
+        weave_rows(nc.vector.tensor_copy, 0, 2, 4)
         for half in range(2):
             quantize_page(1, half * N, (half + 1) * N, wov[half])
+        for a in range(2):
+            gather_v2_words(1, a, "wov%d" % a)
+        gather_v2_scales(1, "page7")
 
-        gather_v2(1)
-        for u in range(4):
+        def scores(u):
             for half in range(2):
                 if u >= 2:
                     score(u, half, 0)
                 score(u, half, 1)
-            e = four.tile([P, T2], F32, name="e", tag="raw", align_bytes=64)
-            if u == 0:
-                nc.scalar.copy(e[:, :N], banks[u][0][:])
-                nc.vector.tensor_copy(e[:, N:], banks[u][1][:])
-            else:
-                for half in range(2):
-                    nc.scalar.copy(e[:, half * N:(half + 1) * N], banks[u][half][:])
-            first = keep.tile([P, N], F32, name="first", tag="x%d" % (4 + u), align_bytes=64)
-            nc.vector.tensor_copy(first[:], e[:].indirect(l_pos1[:]))
-            prod = two.tile([P, N], F32, name="prod", tag="g", align_bytes=64)
-            nc.vector.tensor_tensor(prod[:], e[:].indirect(l_pos2[:]), first[:], ALU.mult)
-            res = keep.tile([P, N], F32, name="res", tag="h%d" % (6 + u % 2), align_bytes=64)
+            e = keep.tile([P, T2], F32, name="e", tag=("raw00", "raw10", "raw01", "raw11")[u], align_bytes=64)
+            for half in range(2):
+                nc.scalar.copy(e[:, half * N:(half + 1) * N], banks[u][half][:])
+            return e
+
+        def first_pick(u):
+            first = keep.tile([P, N], F32, name="first", tag=max_tag[4 + u], align_bytes=64)
+            nc.vector.tensor_copy(first[:], es[u][:].indirect(l_pos1[:]))
+            return first
+
+        def add_closure(u, prod):
+            res = keep.tile([P, N], F32, name="res", tag=("x6", "x7", "x0", "x3")[u], align_bytes=64)
             nc.vector.tensor_tensor(res[:], prod[:], clo[:, u, :], ALU.add)
             nc.sync.dma_start(out[u * P:(u + 1) * P, :], res[:])
+
+        es = [scores(u) for u in range(4)]
+        first = first_pick(0)
+        for u in range(4):
+            prod = two.tile([P, N], F32, name="prod", tag="g", align_bytes=64)
+            nc.vector.tensor_tensor(prod[:], es[u][:].indirect(l_pos2[:]), first[:], ALU.mult)
+            if u < 3:
+                first = first_pick(u + 1)
+            add_closure(u, prod)

@@ -19,9 +19,13 @@ ACT = mybir.ActivationFunctionType
 
 P = 128
 PACK = 4
-KP = 512
+KP = P * PACK
 N = 512
-VECTOR_COLS = 640
+QUAD = 32
+ROW_TILES = H // P
+OUT_TILES = S // P
+CHUNK = T2 // 4
+LINE = 4
 
 
 def tile_list_passage_tie_scores_kernel(tc, tab_words, tab_scales, tab2_words, tab2_scales, w1_words, w1_scales,
@@ -33,39 +37,49 @@ def tile_list_passage_tie_scores_kernel(tc, tab_words, tab_scales, tab2_words, t
         two = ctx.enter_context(tc.tile_pool(name="two", bufs=2))
         psum = ctx.enter_context(tc.psum_pool(name="psum", bufs=2))
 
-        def load_list(src, name):
-            t = keep.tile([P, S // 16], U16, name=name)
-            nc.sync.dma_start(t[:], src)
-            return t
 
-        def load_words(src, pool, name, tag):
-            t = pool.tile([P, T], U32, name=name, tag=tag, align_bytes=64)
-            nc.sync.dma_start(t[:].bitcast(I32), src.rearrange("p n t -> p (n t)").bitcast(I32))
-            return t
+        def load_list(src, name):
+            dst = keep.tile([P, S // 16], U16, name=name)
+            nc.sync.dma_start(dst[:], src)
+            return dst
+
+        def load_words(src, pool, tag):
+            dst = pool.tile([P, T], U32, name="words", tag=tag, align_bytes=64)
+            nc.sync.dma_start(dst[:].bitcast(I32), src.rearrange("p n j -> p (n j)").bitcast(I32))
+            return dst
 
         def load_w2(a, b):
-            t = keep.tile([P, PACK, KP], F32, name="w2raw", tag="raw%d%d" % (a, b), align_bytes=64)
-            nc.sync.dma_start(t[:], w2[a * KP:(a + 1) * KP, b * KP:(b + 1) * KP].rearrange("(p j) c -> p j c", j=PACK))
-            return t
+            dst = keep.tile([P, PACK, KP], F32, name="w2raw", tag="raw%d%d" % (a, b), align_bytes=64)
+            nc.sync.dma_start(dst[:], w2[a * KP:(a + 1) * KP, b * KP:(b + 1) * KP].rearrange("(p j) c -> p j c", j=PACK))
+            return dst
 
         def load_w3(b):
-            t = keep.tile([P, 2, KP], I32, name="w3raw%d" % b, align_bytes=64)
-            src = w3_words.rearrange("a p n t -> p a (n t)")[:, :, b * KP * 4:(b + 1) * KP * 4].bitcast(I32)
-            nc.sync.dma_start(t[:], src)
-            return t
+            dst = keep.tile([P, 2, KP], I32, name="w3raw%d" % b, align_bytes=64)
+            src = w3_words.rearrange("a p n j -> p a (n j)")[:, :, b * KP * 4:(b + 1) * KP * 4].bitcast(I32)
+            nc.sync.dma_start(dst[:], src)
+            return dst
 
         def load_w1(b):
-            t = keep.tile([P, 2, 2 * KP], U8, name="w1raw%d" % b, align_bytes=64)
+            dst = keep.tile([P, 2, 2 * KP], U8, name="w1raw%d" % b, align_bytes=64)
             src = w1_words.rearrange("a p n -> p a n")[:, :, b * KP * 2:(b + 1) * KP * 2].bitcast(I32)
-            nc.sync.dma_start(t[:].bitcast(I32), src)
-            return t
+            nc.sync.dma_start(dst[:].bitcast(I32), src)
+            return dst
 
         page_rows = page0.rearrange("(b p t) n -> b t p n", b=2, t=PACK)
 
         def load_page(i):
-            t = keep.tile([P, T2], F32, name="page%d" % i, align_bytes=64)
-            nc.sync.dma_start(t[:], page_rows[i // PACK, i % PACK])
-            return t
+            dst = keep.tile([P, T2], F32, name="page%d" % i, align_bytes=64)
+            nc.sync.dma_start(dst[:], page_rows[i // PACK, i % PACK])
+            return dst
+
+        def load_scales_beside(dst, src):
+            for q in range(4):
+                nc.sync.dma_start(dst[QUAD * q:QUAD * q + 4, :].bitcast(I32).rearrange("r (a n) -> r a n", a=2),
+                                  src.bitcast(I32)[:, 4 * q:4 * q + 4, :].rearrange("a r n -> r a n"))
+
+        def load_scales_below(dst, src):
+            for q in range(4):
+                nc.sync.dma_start(dst[QUAD * q:QUAD * q + 8, :].bitcast(I32), src.bitcast(I32)[:, 4 * q:4 * q + 4, :])
 
         tabs = keep.tile([P, 2 * T], U8, name="tabs", align_bytes=64)
         w1sraw = keep.tile([P, 2 * H], U8, name="w1sraw", align_bytes=64)
@@ -81,18 +95,9 @@ def tile_list_passage_tie_scores_kernel(tc, tab_words, tab_scales, tab2_words, t
         ident = keep.tile([P, P], F32, name="ident", align_bytes=64)
         make_identity(nc, ident[:])
 
-        def load_scales_beside(dst, src):
-            for q in range(4):
-                nc.sync.dma_start(dst[32 * q:32 * q + 4, :].bitcast(I32).rearrange("r (a n) -> r a n", a=2),
-                                  src.bitcast(I32)[:, 4 * q:4 * q + 4, :].rearrange("a r n -> r a n"))
-
-        def load_scales_below(dst, src):
-            for q in range(4):
-                nc.sync.dma_start(dst[32 * q:32 * q + 8, :].bitcast(I32), src.bitcast(I32)[:, 4 * q:4 * q + 4, :])
-
         tabw = [None, None]
         w2raw = {}
-        tabw[0] = load_words(tab_words[0], two, "tabw", "eightk")
+        tabw[0] = load_words(tab_words[0], two, "eightk")
         load_scales_beside(tabs, tab_scales)
         l_offs = load_list(offs, "l_offs")
         wgs_raw = keep.tile([P, S], F32, name="wgs_raw", align_bytes=64)
@@ -100,7 +105,7 @@ def tile_list_passage_tie_scores_kernel(tc, tab_words, tab_scales, tab2_words, t
         w2raw[0, 0] = load_w2(0, 0)
         load_scales_beside(w1sraw, w1_scales)
         w1raw = [load_w1(0), None]
-        tabw[1] = load_words(tab_words[1], two, "tabw", "eightk")
+        tabw[1] = load_words(tab_words[1], two, "eightk")
         load_scales_below(w3sraw, w3_scales)
         w2raw[1, 0] = load_w2(1, 0)
         w3raw = [load_w3(0), None]
@@ -113,11 +118,11 @@ def tile_list_passage_tie_scores_kernel(tc, tab_words, tab_scales, tab2_words, t
         page.append(load_page(1))
         w2raw[1, 1] = load_w2(1, 1)
         w3raw[1] = load_w3(1)
-        page.extend([load_page(i) for i in range(2, 4)])
+        page.extend([load_page(i) for i in range(2, PACK)])
         l_offs2 = load_list(offs2, "l_offs2")
-        tab2w = [load_words(tab2_words[a], keep, "tab2w%d" % a, "tab2w%d" % a) for a in range(2)]
+        tab2w = [load_words(tab2_words[b], keep, "tab2w%d" % b) for b in range(2)]
         load_scales_below(tab2s, tab2_scales)
-        page.extend([load_page(i) for i in range(4, 8)])
+        page.extend([load_page(i) for i in range(PACK, ROW_TILES)])
         l_pos1 = load_list(pos1, "l_pos1")
         l_pos2 = load_list(pos2, "l_pos2")
 
@@ -130,23 +135,21 @@ def tile_list_passage_tie_scores_kernel(tc, tab_words, tab_scales, tab2_words, t
         w2c = {}
         w2s = {}
 
-        def gather_words(a):
+        def gather_v_words(a):
             nc.vector.tensor_copy(vw[:, a, :], tabw[a][:].indirect(l_offs[:]))
 
-        def gather_scales(a):
+        def gather_v_scales(a):
             nc.vector.tensor_copy(vs[:, a, :], tabs[:, a * T:(a + 1) * T].indirect(l_offs[:]))
 
-        def round_w2(a, b, tag):
-            g = keep.tile([P, PACK, P, PACK], BF16, name="w2bf", tag=tag, align_bytes=64)
-            dst = g[:].rearrange("p t m j -> p m j t")
-            src = w2raw[a, b][:].rearrange("p j (m t) -> p m j t", t=PACK)
-            nc.scalar.copy(dst, src)
-            return g
+        def round_w2(a, b, copy, tag):
+            rounded = keep.tile([P, PACK, P, PACK], BF16, name="w2bf", tag=tag, align_bytes=64)
+            copy(rounded[:].rearrange("p t m j -> p m j t"), w2raw[a, b][:].rearrange("p j (m t) -> p m j t", t=PACK))
+            return rounded
 
-        def quantize_w2(a, b, g, cuts, tag):
+        def quantize_w2(a, b, rounded, cuts, tag):
             w2c[a, b] = keep.tile([P, KP], U32, name="w2c", tag=tag, align_bytes=64)
             w2s[a, b] = keep.tile([P, KP], U8, name="w2s%d%d" % (a, b), align_bytes=64)
-            flat = g[:].rearrange("p t m j -> p (t m j)")
+            flat = rounded[:].rearrange("p t m j -> p (t m j)")
             for lo, hi in cuts:
                 nc.vector.quantize_mx(out=w2c[a, b][:, lo:hi].bitcast(FP8X4), scales=w2s[a, b][:, lo:hi],
                                       in_=flat[:, PACK * lo:PACK * hi])
@@ -164,20 +167,21 @@ def tile_list_passage_tie_scores_kernel(tc, tab_words, tab_scales, tab2_words, t
             nc.vector.tensor_copy(w3p[b][:].bitcast(I32).rearrange("p a (t m) -> p a m t", t=PACK),
                                   w3raw[b][:].rearrange("p a (m t) -> p a m t", t=PACK))
 
-        gather_words(0)
-        gather_scales(0)
-        gather_scales(1)
+        gather_v_words(0)
+        gather_v_scales(0)
+        gather_v_scales(1)
         deal_w1(0)
         deal_scales(w1sp, w1sraw)
-        g00 = round_w2(0, 0, "wov0")
-        gather_words(1)
-        quantize_w2(0, 0, g00, [(0, KP)], "w2c00")
+        rounded00 = round_w2(0, 0, nc.scalar.copy, "wov0")
+        gather_v_words(1)
+        quantize_w2(0, 0, rounded00, [(0, KP)], "w2c00")
         deal_scales(w3sp, w3sraw)
-        g10 = round_w2(1, 0, "x1")
+        rounded10 = round_w2(1, 0, nc.vector.tensor_copy, "wov1")
         deal_w3(0, "w3p0")
-        quantize_w2(1, 0, g10, [(0, P), (P, KP)], "w3raw0")
+        quantize_w2(1, 0, rounded10, [(0, P), (P, KP)], "w3raw0")
 
-        def product(tag, i, lhs, lhs_scale):
+
+        def product(tag, lhs, lhs_scale):
             acc = psum.tile([P, N], F32, name=tag, tag=tag)
             for a in range(2):
                 nc.tensor.matmul_mx(out=acc[:], lhsT=lhs(a), lhsT_scale=lhs_scale(a), rhs=vw[:, a, :].bitcast(FP8X4),
@@ -189,27 +193,27 @@ def tile_list_passage_tie_scores_kernel(tc, tab_words, tab_scales, tab2_words, t
         def gated(i):
             b, t = divmod(i, PACK)
             tags = ("pa", "pb") if i // 2 % 2 == 0 else ("pb", "pa")
-            pa = product(tags[0], i, lambda a: w1p[b][:, a, 2 * t * P:2 * (t + 1) * P].bitcast(FP4X4),
-                         lambda a: w1sp[:, a * H + i * P:a * H + (i + 1) * P])
-            pb = product(tags[1], i, lambda a: w2c[a, b][:, t * P:(t + 1) * P].bitcast(FP8X4),
-                         lambda a: w2s[a, b][:, t * P:(t + 1) * P])
-            xa = keep.tile([P, N], F32, name="xa", tag={0: "raw10", 4: "h3"}.get(i, "x%d" % i), align_bytes=64)
-            x = keep.tile([P, N], F32, name="x", tag=max_tag[i], align_bytes=64) if i in (4, 6, 7) else xa
-            nc.scalar.copy(xa[:], pa[:])
-            nc.vector.tensor_tensor(x[:], xa[:], pb[:], ALU.max)
-            g = two.tile([P, N], F32, name="g", tag="g", align_bytes=64)
-            nc.scalar.activation(g[:], x[:], ACT.Gelu_apprx_tanh)
-            return g
+            sum1 = product(tags[0], lambda a: w1p[b][:, a, 2 * t * P:2 * (t + 1) * P].bitcast(FP4X4),
+                           lambda a: w1sp[:, a * H + i * P:a * H + (i + 1) * P])
+            sum2 = product(tags[1], lambda a: w2c[a, b][:, t * P:(t + 1) * P].bitcast(FP8X4),
+                           lambda a: w2s[a, b][:, t * P:(t + 1) * P])
+            copied = keep.tile([P, N], F32, name="copied", tag="h3" if i == PACK else "x%d" % i, align_bytes=64)
+            larger = keep.tile([P, N], F32, name="larger", tag=max_tag[i], align_bytes=64) if i in (4, 6, 7) else copied
+            nc.scalar.copy(copied[:], sum1[:])
+            nc.vector.tensor_tensor(larger[:], copied[:], sum2[:], ALU.max)
+            act = two.tile([P, N], F32, name="act", tag="g", align_bytes=64)
+            nc.scalar.activation(act[:], larger[:], ACT.Gelu_apprx_tanh)
+            return act
 
         def linear(i):
             b, t = divmod(i, PACK)
-            return product("pc", i, lambda a: w3p[b][:, a, t * P:(t + 1) * P].bitcast(FP8X4),
+            return product("pc", lambda a: w3p[b][:, a, t * P:(t + 1) * P].bitcast(FP8X4),
                            lambda a: w3sp[4 * a:P, i * P:(i + 1) * P])
 
-        def combine(i, g, pc):
+        def combine(i, act, sum3):
             b, t = divmod(i, PACK)
             h = keep.tile([P, N], F32, name="h", tag={1: "x1", 2: "x2"}.get(i, "h%d" % i), align_bytes=64)
-            nc.vector.scalar_tensor_tensor(h[:], g[:], gain_sb[:, b, t:t + 1], pc[:], ALU.mult, ALU.add)
+            nc.vector.scalar_tensor_tensor(h[:], act[:], gain_sb[:, b, t:t + 1], sum3[:], ALU.mult, ALU.add)
             return h
 
         def put(i, h):
@@ -217,110 +221,112 @@ def tile_list_passage_tie_scores_kernel(tc, tab_words, tab_scales, tab2_words, t
 
         pcodes = [keep.tile([P, T2], U32, name="pcodes%d" % b, align_bytes=64) for b in range(2)]
         pscales = [keep.tile([P, T2], U8, name="pscales%d" % b, align_bytes=64) for b in range(2)]
-
-        def weave(copy, dst, planes, lo, hi):
-            copy(dst.rearrange("p (c i) t -> p c t i", i=4), planes[:, :, lo:hi].rearrange("p t (c i) -> p c t i", i=4))
+        rows16 = [None, None]
+        v2w = {}
+        v2s = {}
 
         def quantize_page(b, lo, hi, woven):
             nc.vector.quantize_mx(out=pcodes[b][:, lo:hi].bitcast(FP8X4), scales=pscales[b][:, lo:hi],
                                   in_=woven[:].rearrange("p n t -> p (n t)"))
 
-        planes = [None, None]
+        def weave_chunk(c, tag):
+            lo, hi = c * CHUNK, (c + 1) * CHUNK
+            woven = keep.tile([P, CHUNK, PACK], BF16, name="woven", tag=tag, align_bytes=64)
+            nc.scalar.copy(woven[:].rearrange("p (n e) t -> p n t e", e=LINE),
+                           rows16[0][:, :, lo:hi].rearrange("p t (n e) -> p n t e", e=LINE))
+            quantize_page(0, lo, hi, woven)
 
-        v2w = {}
-        v2s = {}
+        def weave_rows(copy, half, lo, hi):
+            copy(wov[half][:, :, lo:hi], rows16[1][:, lo:hi, half * N:(half + 1) * N].rearrange("p t n -> p n t"))
 
-        def gather_v2_words(part, a, tag):
-            v2w[part, a] = keep.tile([P, S // 2], U32, name="v2w", tag=tag, align_bytes=64)
-            nc.vector.tensor_copy(v2w[part, a][:], tab2w[a][:].indirect(l_offs2[:, part * 16:(part + 1) * 16]))
+        def gather_v2_words(part, b, tag):
+            v2w[part, b] = keep.tile([P, S // 2], U32, name="v2w", tag=tag, align_bytes=64)
+            nc.vector.tensor_copy(v2w[part, b][:], tab2w[b][:].indirect(l_offs2[:, part * 16:(part + 1) * 16]))
 
         def gather_v2_scales(part, tag):
             v2s[part] = keep.tile([P, S // 2], U8, name="v2s", tag=tag, align_bytes=64)
             nc.vector.tensor_copy(v2s[part][:], tab2s[:].indirect(l_offs2[:, part * 16:(part + 1) * 16]))
 
-        def weave_rows(copy, half, lo, hi):
-            copy(wov[half][:, :, lo:hi], planes[1][:, lo:hi, half * N:(half + 1) * N].rearrange("p t n -> p n t"))
 
         def turn(dst, src):
-            for k in range(4):
+            for k in range(N // P):
                 nc.tensor.transpose(dst[:, k * P:(k + 1) * P], src[:, k * P:(k + 1) * P], ident[:])
 
-        def spread_wgs(t):
-            rep = keep.tile([P, 4, 4, 32], F32, name="rep", tag="rep" if t < 3 else "page0", align_bytes=64)
-            rows = wgs_t[:].rearrange("p (k q t) -> p k q t", k=4, t=PACK)[:, :, :, t]
-            nc.scalar.copy(rep[:], rows.unsqueeze(2).to_broadcast([P, 4, 4, 32]))
+        def spread_wgs(t, tag):
+            rep = keep.tile([P, S // P, P // QUAD, QUAD], F32, name="rep", tag=tag, align_bytes=64)
+            picked = wgs_t[:].rearrange("p (k q t) -> p k q t", k=S // P, t=PACK)[:, :, :, t]
+            nc.scalar.copy(rep[:], picked.unsqueeze(2).to_broadcast([P, S // P, P // QUAD, QUAD]))
             back = psum.tile([P, N], F32, name="back", tag="back", bufs=1)
             turn(back, rep[:].rearrange("p k c q -> p (k c q)"))
-            dealt = keep.tile([P, S], F32, name="wgs%d" % t, align_bytes=64)
-            nc.scalar.copy(dealt[:], back[:])
-            return dealt[:]
+            spread = keep.tile([P, S], F32, name="wgs%d" % t, align_bytes=64)
+            nc.scalar.copy(spread[:], back[:])
+            return spread[:]
 
         wgs_t = psum.tile([P, N], F32, name="wgs_t", tag="fore", bufs=1)
         turn(wgs_t, wgs_raw)
-        wgs_sb = [spread_wgs(t) for t in range(3)]
-        gs = [gated(0)]
-        pcs = [linear(0)]
-        gs.append(gated(1))
-        pcs.append(linear(1))
+        wgs_sb = [spread_wgs(t, "rep") for t in range(PACK - 1)]
+
+        acts = [gated(0)]
+        sums3 = [linear(0)]
+        acts.append(gated(1))
+        sums3.append(linear(1))
         deal_w1(1)
         wov = [keep.tile([P, N, PACK], BF16, name="wov", tag="wov%d" % half, align_bytes=64) for half in range(2)]
-        for i in range(8):
+        for i in range(ROW_TILES):
             b, t = divmod(i, PACK)
-            if i == 1:
-                quantize_w2(0, 1, round_w2(0, 1, "x1"), [(0, KP)], "h0")
+            if i in (1, 2):
+                quantize_w2(i - 1, 1, round_w2(i - 1, 1, nc.scalar.copy, "x%d" % i), [(0, KP)], ("h0", "x1")[i - 1])
             if i == 2:
-                quantize_w2(1, 1, round_w2(1, 1, "x2"), [(0, KP)], "x1")
-                planes[0] = keep.tile([P, PACK, T2], BF16, name="planes0", tag="raw11", align_bytes=64)
-                nc.scalar.copy(planes[0][:, 0, :], page[0][:])
-                wgs_sb.append(spread_wgs(3))
-                nc.scalar.copy(planes[0][:, 1, :], page[1][:])
-            h = combine(i, gs[i], pcs[i])
+                rows16[0] = keep.tile([P, PACK, T2], BF16, name="rows16", tag="raw11", align_bytes=64)
+                nc.scalar.copy(rows16[0][:, 0, :], page[0][:])
+                wgs_sb.append(spread_wgs(PACK - 1, "page0"))
+                nc.scalar.copy(rows16[0][:, 1, :], page[1][:])
+            h = combine(i, acts[i], sums3[i])
             if i == 2:
                 deal_w3(1, "page1")
-            if i + 2 < 8:
-                gs.append(gated(i + 2))
-                pcs.append(linear(i + 2))
+            if i + 2 < ROW_TILES:
+                acts.append(gated(i + 2))
+                sums3.append(linear(i + 2))
             else:
-                gather_v2_words(0, i - 6, "h%d" % (i - 1))
+                gather_v2_words(0, i + 2 - ROW_TILES, "h%d" % (i - 1))
             put(i, h)
-            if i == 4:
-                planes[1] = two.tile([P, PACK, T2], BF16, name="planes1", tag="eightk", align_bytes=64)
-            if 2 <= i < 7:
-                nc.scalar.copy(planes[b][:, t, :], page[i][:])
-            if 3 <= i < 7:
-                lo = (i - 3) * 256
-                woven = keep.tile([P, 256, PACK], BF16, name="woven", tag=max_tag[i + 1], align_bytes=64)
-                weave(nc.scalar.copy, woven[:], planes[0], lo, lo + 256)
-                quantize_page(0, lo, lo + 256, woven)
-            if i == 5:
+            if i == PACK:
+                rows16[1] = two.tile([P, PACK, T2], BF16, name="rows16", tag="eightk", align_bytes=64)
+            if 2 <= i < ROW_TILES - 1:
+                nc.scalar.copy(rows16[b][:, t, :], page[i][:])
+            if PACK - 1 <= i < ROW_TILES - 1:
+                weave_chunk(i - (PACK - 1), max_tag[i + 1])
+            if i == PACK + 1:
                 gather_v2_scales(0, "page4")
                 weave_rows(nc.scalar.copy, 0, 0, 2)
-            if i == 6:
+            if i == PACK + 2:
                 weave_rows(nc.scalar.copy, 1, 0, 3)
 
-        clo = two.tile([P, 4, N], F32, name="clo", tag="eightk", align_bytes=64)
+        clo = two.tile([P, OUT_TILES, N], F32, name="clo", tag="eightk", align_bytes=64)
         nc.sync.dma_start(clo[:], closure.rearrange("(u p) j -> p u j", p=P))
 
         banks = [[psum.tile([P, N], F32, name="bank", tag=tag, bufs=1) for tag in ("fore", "back")]]
         banks.extend([[psum.tile([P, N], F32, name="bank", tag=tag) for half in range(2)] for tag in ("pa", "pb", "pc")])
 
         def score(u, half, b):
+            part, cand = u // 2, slice(u % 2 * P, (u % 2 + 1) * P)
             cols = slice(half * N, (half + 1) * N)
-            nc.tensor.matmul_mx(out=banks[u][half][:], lhsT=v2w[u // 2, b][:, u % 2 * P:(u % 2 + 1) * P].bitcast(FP8X4),
-                                lhsT_scale=v2s[u // 2][4 * b:P, u % 2 * P:(u % 2 + 1) * P], rhs=pcodes[b][:, cols].bitcast(FP8X4),
+            nc.tensor.matmul_mx(out=banks[u][half][:], lhsT=v2w[part, b][:, cand].bitcast(FP8X4),
+                                lhsT_scale=v2s[part][4 * b:P, cand], rhs=pcodes[b][:, cols].bitcast(FP8X4),
                                 rhs_scale=pscales[b][:, cols], start=(b == 0), stop=(b == 1))
 
         for u in range(2):
             for half in range(2):
                 score(u, half, 0)
 
-        nc.scalar.copy(wov[1][:, :, 3], page[7][:, N:])
-        nc.vector.tensor_copy(planes[1][:, 3, :N], page[7][:, :N])
-        weave_rows(nc.vector.tensor_copy, 0, 2, 4)
+        last = page[ROW_TILES - 1]
+        nc.scalar.copy(wov[1][:, :, PACK - 1], last[:, N:])
+        nc.vector.tensor_copy(rows16[1][:, PACK - 1, :N], last[:, :N])
+        weave_rows(nc.vector.tensor_copy, 0, 2, PACK)
         for half in range(2):
             quantize_page(1, half * N, (half + 1) * N, wov[half])
-        for a in range(2):
-            gather_v2_words(1, a, "wov%d" % a)
+        for b in range(2):
+            gather_v2_words(1, b, "wov%d" % b)
         gather_v2_scales(1, "page7")
 
         def scores(u):
@@ -334,7 +340,7 @@ def tile_list_passage_tie_scores_kernel(tc, tab_words, tab_scales, tab2_words, t
             return e
 
         def first_pick(u):
-            first = keep.tile([P, N], F32, name="first", tag=max_tag[4 + u], align_bytes=64)
+            first = keep.tile([P, N], F32, name="first", tag=max_tag[PACK + u], align_bytes=64)
             nc.vector.tensor_copy(first[:], es[u][:].indirect(l_pos1[:]))
             return first
 
@@ -343,11 +349,11 @@ def tile_list_passage_tie_scores_kernel(tc, tab_words, tab_scales, tab2_words, t
             nc.vector.tensor_tensor(res[:], prod[:], clo[:, u, :], ALU.add)
             nc.sync.dma_start(out[u * P:(u + 1) * P, :], res[:])
 
-        es = [scores(u) for u in range(4)]
-        first = first_pick(0)
-        for u in range(4):
+        es = [scores(u) for u in range(OUT_TILES)]
+        picked1 = first_pick(0)
+        for u in range(OUT_TILES):
             prod = two.tile([P, N], F32, name="prod", tag="g", align_bytes=64)
-            nc.vector.tensor_tensor(prod[:], es[u][:].indirect(l_pos2[:]), first[:], ALU.mult)
-            if u < 3:
-                first = first_pick(u + 1)
+            nc.vector.tensor_tensor(prod[:], es[u][:].indirect(l_pos2[:]), picked1[:], ALU.mult)
+            if u + 1 < OUT_TILES:
+                picked1 = first_pick(u + 1)
             add_closure(u, prod)

from contextlib import ExitStack

import concourse.mybir as mybir
from concourse.masks import make_identity

K, H, T, S, T2 = 1024, 1024, 2048, 512, 1024
FLOPS = 3 * 2 * K * H * S + 2 * H * S * T2

F32 = mybir.dt.float32
BF16 = mybir.dt.bfloat16
I32 = mybir.dt.int32
U32 = mybir.dt.uint32
U16 = mybir.dt.uint16
U8 = mybir.dt.uint8
FP8X4 = mybir.dt.float8_e4m3fn_x4
FP4X4 = mybir.dt.float4_e2m1fn_x4
ALU = mybir.AluOpType
ACT = mybir.ActivationFunctionType

P = 128
PACK = 4
KP = P * PACK
N = 512
QUAD = 32
ROW_TILES = H // P
OUT_TILES = S // P
CHUNK = T2 // 4
LINE = 4


def tile_list_passage_tie_scores_kernel(tc, tab_words, tab_scales, tab2_words, tab2_scales, w1_words, w1_scales,
                                                  w2, w3_words, w3_scales, gain, wgs, page0, closure,
                                                  offs, offs2, offs3, pos1, pos2, out):
    nc = tc.nc
    with ExitStack() as ctx:
        keep = ctx.enter_context(tc.tile_pool(name="keep", bufs=1))
        two = ctx.enter_context(tc.tile_pool(name="two", bufs=2))
        psum = ctx.enter_context(tc.psum_pool(name="psum", bufs=2))


        def load_list(src, name):
            dst = keep.tile([P, S // 16], U16, name=name)
            nc.sync.dma_start(dst[:], src)
            return dst

        def load_words(src, pool, tag):
            dst = pool.tile([P, T], U32, name="words", tag=tag, align_bytes=64)
            nc.sync.dma_start(dst[:].bitcast(I32), src.rearrange("p n j -> p (n j)").bitcast(I32))
            return dst

        def load_w2(a, b):
            dst = keep.tile([P, PACK, KP], F32, name="w2raw", tag="raw%d%d" % (a, b), align_bytes=64)
            nc.sync.dma_start(dst[:], w2[a * KP:(a + 1) * KP, b * KP:(b + 1) * KP].rearrange("(p j) c -> p j c", j=PACK))
            return dst

        def load_w3(b):
            dst = keep.tile([P, 2, KP], I32, name="w3raw%d" % b, align_bytes=64)
            src = w3_words.rearrange("a p n j -> p a (n j)")[:, :, b * KP * 4:(b + 1) * KP * 4].bitcast(I32)
            nc.sync.dma_start(dst[:], src)
            return dst

        def load_w1(b):
            dst = keep.tile([P, 2, 2 * KP], U8, name="w1raw%d" % b, align_bytes=64)
            src = w1_words.rearrange("a p n -> p a n")[:, :, b * KP * 2:(b + 1) * KP * 2].bitcast(I32)
            nc.sync.dma_start(dst[:].bitcast(I32), src)
            return dst

        page_rows = page0.rearrange("(b p t) n -> b t p n", b=2, t=PACK)

        def load_page(i):
            dst = keep.tile([P, T2], F32, name="page%d" % i, align_bytes=64)
            nc.sync.dma_start(dst[:], page_rows[i // PACK, i % PACK])
            return dst

        def load_scales_beside(dst, src):
            for q in range(4):
                nc.sync.dma_start(dst[QUAD * q:QUAD * q + 4, :].bitcast(I32).rearrange("r (a n) -> r a n", a=2),
                                  src.bitcast(I32)[:, 4 * q:4 * q + 4, :].rearrange("a r n -> r a n"))

        def load_scales_below(dst, src):
            for q in range(4):
                nc.sync.dma_start(dst[QUAD * q:QUAD * q + 8, :].bitcast(I32), src.bitcast(I32)[:, 4 * q:4 * q + 4, :])

        tabs = keep.tile([P, 2 * T], U8, name="tabs", align_bytes=64)
        w1sraw = keep.tile([P, 2 * H], U8, name="w1sraw", align_bytes=64)
        w3sraw = keep.tile([P, H], U8, name="w3sraw", align_bytes=64)
        tab2s = keep.tile([P, T], U8, name="tab2s", align_bytes=64)
        nc.vector.memset(tabs[:].bitcast(I32), 0)
        warm = keep.tile([P, 2], F32, name="warm")
        nc.gpsimd.memset(warm[:, 0:1], 0.0)
        nc.scalar.activation(warm[:, 1:2], warm[:, 0:1], ACT.Gelu_apprx_tanh)
        nc.gpsimd.memset(w1sraw[:].bitcast(I32), 0)
        nc.gpsimd.memset(w3sraw[:].bitcast(I32), 0)
        nc.gpsimd.memset(tab2s[:].bitcast(I32), 0)
        ident = keep.tile([P, P], F32, name="ident", align_bytes=64)
        make_identity(nc, ident[:])

        tabw = [None, None]
        w2raw = {}
        tabw[0] = load_words(tab_words[0], two, "eightk")
        load_scales_beside(tabs, tab_scales)
        l_offs = load_list(offs, "l_offs")
        wgs_raw = keep.tile([P, S], F32, name="wgs_raw", align_bytes=64)
        nc.sync.dma_start(wgs_raw[:], wgs)
        w2raw[0, 0] = load_w2(0, 0)
        load_scales_beside(w1sraw, w1_scales)
        w1raw = [load_w1(0), None]
        tabw[1] = load_words(tab_words[1], two, "eightk")
        load_scales_below(w3sraw, w3_scales)
        w2raw[1, 0] = load_w2(1, 0)
        w3raw = [load_w3(0), None]
        gain_sb = keep.tile([P, 2, PACK], F32, name="gain_sb")
        nc.sync.dma_start(gain_sb[:], gain.rearrange("(b p t) -> p b t", b=2, t=PACK))
        l_offs3 = load_list(offs3, "l_offs3")
        page = [load_page(0)]
        w1raw[1] = load_w1(1)
        w2raw[0, 1] = load_w2(0, 1)
        page.append(load_page(1))
        w2raw[1, 1] = load_w2(1, 1)
        w3raw[1] = load_w3(1)
        page.extend([load_page(i) for i in range(2, PACK)])
        l_offs2 = load_list(offs2, "l_offs2")
        tab2w = [load_words(tab2_words[b], keep, "tab2w%d" % b) for b in range(2)]
        load_scales_below(tab2s, tab2_scales)
        page.extend([load_page(i) for i in range(PACK, ROW_TILES)])
        l_pos1 = load_list(pos1, "l_pos1")
        l_pos2 = load_list(pos2, "l_pos2")

        vw = keep.tile([P, 2, S], U32, name="vw", align_bytes=64)
        vs = keep.tile([P, 2, S], U8, name="vs", align_bytes=64)
        w1p = [keep.tile([P, 2, 2 * KP], U8, name="w1p%d" % b, align_bytes=64) for b in range(2)]
        w1sp = keep.tile([P, 2 * H], U8, name="w1sp", align_bytes=64)
        w3sp = keep.tile([P, H], U8, name="w3sp", align_bytes=64)
        w3p = [None, None]
        w2c = {}
        w2s = {}

        def gather_v_words(a):
            nc.vector.tensor_copy(vw[:, a, :], tabw[a][:].indirect(l_offs[:]))

        def gather_v_scales(a):
            nc.vector.tensor_copy(vs[:, a, :], tabs[:, a * T:(a + 1) * T].indirect(l_offs[:]))

        def round_w2(a, b, copy, tag):
            rounded = keep.tile([P, PACK, P, PACK], BF16, name="w2bf", tag=tag, align_bytes=64)
            copy(rounded[:].rearrange("p t m j -> p m j t"), w2raw[a, b][:].rearrange("p j (m t) -> p m j t", t=PACK))
            return rounded

        def quantize_w2(a, b, rounded, cuts, tag):
            w2c[a, b] = keep.tile([P, KP], U32, name="w2c", tag=tag, align_bytes=64)
            w2s[a, b] = keep.tile([P, KP], U8, name="w2s%d%d" % (a, b), align_bytes=64)
            flat = rounded[:].rearrange("p t m j -> p (t m j)")
            for lo, hi in cuts:
                nc.vector.quantize_mx(out=w2c[a, b][:, lo:hi].bitcast(FP8X4), scales=w2s[a, b][:, lo:hi],
                                      in_=flat[:, PACK * lo:PACK * hi])

        def deal_scales(dst, src):
            nc.vector.tensor_copy(dst[:].rearrange("p (g t m) -> p g t m", t=PACK, m=P),
                                  src[:].rearrange("p (g m t) -> p g t m", t=PACK, m=P))

        def deal_w1(b):
            nc.vector.tensor_copy(w1p[b][:].bitcast(U16).rearrange("p a (t m) -> p a t m", t=PACK),
                                  w1raw[b][:].bitcast(U16).rearrange("p a (m t) -> p a t m", t=PACK))

        def deal_w3(b, tag):
            w3p[b] = keep.tile([P, 2, KP], U32, name="w3p", tag=tag, align_bytes=64)
            nc.vector.tensor_copy(w3p[b][:].bitcast(I32).rearrange("p a (t m) -> p a m t", t=PACK),
                                  w3raw[b][:].rearrange("p a (m t) -> p a m t", t=PACK))

        gather_v_words(0)
        gather_v_scales(0)
        gather_v_scales(1)
        deal_w1(0)
        deal_scales(w1sp, w1sraw)
        rounded00 = round_w2(0, 0, nc.scalar.copy, "wov0")
        gather_v_words(1)
        quantize_w2(0, 0, rounded00, [(0, KP)], "w2c00")
        deal_scales(w3sp, w3sraw)
        rounded10 = round_w2(1, 0, nc.vector.tensor_copy, "wov1")
        deal_w3(0, "w3p0")
        quantize_w2(1, 0, rounded10, [(0, P), (P, KP)], "w3raw0")


        def product(tag, lhs, lhs_scale):
            acc = psum.tile([P, N], F32, name=tag, tag=tag)
            for a in range(2):
                nc.tensor.matmul_mx(out=acc[:], lhsT=lhs(a), lhsT_scale=lhs_scale(a), rhs=vw[:, a, :].bitcast(FP8X4),
                                    rhs_scale=vs[:, a, :], start=(a == 0), stop=(a == 1))
            return acc

        max_tag = {4: "x4", 5: "x5", 6: "h3", 7: "h4"}

        def gated(i):
            b, t = divmod(i, PACK)
            tags = ("pa", "pb") if i // 2 % 2 == 0 else ("pb", "pa")
            sum1 = product(tags[0], lambda a: w1p[b][:, a, 2 * t * P:2 * (t + 1) * P].bitcast(FP4X4),
                           lambda a: w1sp[:, a * H + i * P:a * H + (i + 1) * P])
            sum2 = product(tags[1], lambda a: w2c[a, b][:, t * P:(t + 1) * P].bitcast(FP8X4),
                           lambda a: w2s[a, b][:, t * P:(t + 1) * P])
            copied = keep.tile([P, N], F32, name="copied", tag="h3" if i == PACK else "x%d" % i, align_bytes=64)
            larger = keep.tile([P, N], F32, name="larger", tag=max_tag[i], align_bytes=64) if i in (4, 6, 7) else copied
            nc.scalar.copy(copied[:], sum1[:])
            nc.vector.tensor_tensor(larger[:], copied[:], sum2[:], ALU.max)
            act = two.tile([P, N], F32, name="act", tag="g", align_bytes=64)
            nc.scalar.activation(act[:], larger[:], ACT.Gelu_apprx_tanh)
            return act

        def linear(i):
            b, t = divmod(i, PACK)
            return product("pc", lambda a: w3p[b][:, a, t * P:(t + 1) * P].bitcast(FP8X4),
                           lambda a: w3sp[4 * a:P, i * P:(i + 1) * P])

        def combine(i, act, sum3):
            b, t = divmod(i, PACK)
            h = keep.tile([P, N], F32, name="h", tag={1: "x1", 2: "x2"}.get(i, "h%d" % i), align_bytes=64)
            nc.vector.scalar_tensor_tensor(h[:], act[:], gain_sb[:, b, t:t + 1], sum3[:], ALU.mult, ALU.add)
            return h

        def put(i, h):
            nc.vector.tensor_tensor(page[i][:].indirect(l_offs3[:]), h[:], wgs_sb[i % PACK], ALU.mult)

        pcodes = [keep.tile([P, T2], U32, name="pcodes%d" % b, align_bytes=64) for b in range(2)]
        pscales = [keep.tile([P, T2], U8, name="pscales%d" % b, align_bytes=64) for b in range(2)]
        rows16 = [None, None]
        v2w = {}
        v2s = {}

        def quantize_page(b, lo, hi, woven):
            nc.vector.quantize_mx(out=pcodes[b][:, lo:hi].bitcast(FP8X4), scales=pscales[b][:, lo:hi],
                                  in_=woven[:].rearrange("p n t -> p (n t)"))

        def weave_chunk(c, tag):
            lo, hi = c * CHUNK, (c + 1) * CHUNK
            woven = keep.tile([P, CHUNK, PACK], BF16, name="woven", tag=tag, align_bytes=64)
            nc.scalar.copy(woven[:].rearrange("p (n e) t -> p n t e", e=LINE),
                           rows16[0][:, :, lo:hi].rearrange("p t (n e) -> p n t e", e=LINE))
            quantize_page(0, lo, hi, woven)

        def weave_rows(copy, half, lo, hi):
            copy(wov[half][:, :, lo:hi], rows16[1][:, lo:hi, half * N:(half + 1) * N].rearrange("p t n -> p n t"))

        def gather_v2_words(part, b, tag):
            v2w[part, b] = keep.tile([P, S // 2], U32, name="v2w", tag=tag, align_bytes=64)
            nc.vector.tensor_copy(v2w[part, b][:], tab2w[b][:].indirect(l_offs2[:, part * 16:(part + 1) * 16]))

        def gather_v2_scales(part, tag):
            v2s[part] = keep.tile([P, S // 2], U8, name="v2s", tag=tag, align_bytes=64)
            nc.vector.tensor_copy(v2s[part][:], tab2s[:].indirect(l_offs2[:, part * 16:(part + 1) * 16]))


        def turn(dst, src):
            for k in range(N // P):
                nc.tensor.transpose(dst[:, k * P:(k + 1) * P], src[:, k * P:(k + 1) * P], ident[:])

        def spread_wgs(t, tag):
            rep = keep.tile([P, S // P, P // QUAD, QUAD], F32, name="rep", tag=tag, align_bytes=64)
            picked = wgs_t[:].rearrange("p (k q t) -> p k q t", k=S // P, t=PACK)[:, :, :, t]
            nc.scalar.copy(rep[:], picked.unsqueeze(2).to_broadcast([P, S // P, P // QUAD, QUAD]))
            back = psum.tile([P, N], F32, name="back", tag="back", bufs=1)
            turn(back, rep[:].rearrange("p k c q -> p (k c q)"))
            spread = keep.tile([P, S], F32, name="wgs%d" % t, align_bytes=64)
            nc.scalar.copy(spread[:], back[:])
            return spread[:]

        wgs_t = psum.tile([P, N], F32, name="wgs_t", tag="fore", bufs=1)
        turn(wgs_t, wgs_raw)
        wgs_sb = [spread_wgs(t, "rep") for t in range(PACK - 1)]

        acts = [gated(0)]
        sums3 = [linear(0)]
        acts.append(gated(1))
        sums3.append(linear(1))
        deal_w1(1)
        wov = [keep.tile([P, N, PACK], BF16, name="wov", tag="wov%d" % half, align_bytes=64) for half in range(2)]
        for i in range(ROW_TILES):
            b, t = divmod(i, PACK)
            if i in (1, 2):
                quantize_w2(i - 1, 1, round_w2(i - 1, 1, nc.scalar.copy, "x%d" % i), [(0, KP)], ("h0", "x1")[i - 1])
            if i == 2:
                rows16[0] = keep.tile([P, PACK, T2], BF16, name="rows16", tag="raw11", align_bytes=64)
                nc.scalar.copy(rows16[0][:, 0, :], page[0][:])
                wgs_sb.append(spread_wgs(PACK - 1, "page0"))
                nc.scalar.copy(rows16[0][:, 1, :], page[1][:])
            h = combine(i, acts[i], sums3[i])
            if i == 2:
                deal_w3(1, "page1")
            if i + 2 < ROW_TILES:
                acts.append(gated(i + 2))
                sums3.append(linear(i + 2))
            else:
                gather_v2_words(0, i + 2 - ROW_TILES, "h%d" % (i - 1))
            put(i, h)
            if i == PACK:
                rows16[1] = two.tile([P, PACK, T2], BF16, name="rows16", tag="eightk", align_bytes=64)
            if 2 <= i < ROW_TILES - 1:
                nc.scalar.copy(rows16[b][:, t, :], page[i][:])
            if PACK - 1 <= i < ROW_TILES - 1:
                weave_chunk(i - (PACK - 1), max_tag[i + 1])
            if i == PACK + 1:
                gather_v2_scales(0, "page4")
                weave_rows(nc.scalar.copy, 0, 0, 2)
            if i == PACK + 2:
                weave_rows(nc.scalar.copy, 1, 0, 3)

        clo = two.tile([P, OUT_TILES, N], F32, name="clo", tag="eightk", align_bytes=64)
        nc.sync.dma_start(clo[:], closure.rearrange("(u p) j -> p u j", p=P))

        banks = [[psum.tile([P, N], F32, name="bank", tag=tag, bufs=1) for tag in ("fore", "back")]]
        banks.extend([[psum.tile([P, N], F32, name="bank", tag=tag) for half in range(2)] for tag in ("pa", "pb", "pc")])

        def score(u, half, b):
            part, cand = u // 2, slice(u % 2 * P, (u % 2 + 1) * P)
            cols = slice(half * N, (half + 1) * N)
            nc.tensor.matmul_mx(out=banks[u][half][:], lhsT=v2w[part, b][:, cand].bitcast(FP8X4),
                                lhsT_scale=v2s[part][4 * b:P, cand], rhs=pcodes[b][:, cols].bitcast(FP8X4),
                                rhs_scale=pscales[b][:, cols], start=(b == 0), stop=(b == 1))

        for u in range(2):
            for half in range(2):
                score(u, half, 0)

        last = page[ROW_TILES - 1]
        nc.scalar.copy(wov[1][:, :, PACK - 1], last[:, N:])
        nc.vector.tensor_copy(rows16[1][:, PACK - 1, :N], last[:, :N])
        weave_rows(nc.vector.tensor_copy, 0, 2, PACK)
        for half in range(2):
            quantize_page(1, half * N, (half + 1) * N, wov[half])
        for b in range(2):
            gather_v2_words(1, b, "wov%d" % b)
        gather_v2_scales(1, "page7")

        def scores(u):
            for half in range(2):
                if u >= 2:
                    score(u, half, 0)
                score(u, half, 1)
            e = keep.tile([P, T2], F32, name="e", tag=("raw00", "raw10", "raw01", "raw11")[u], align_bytes=64)
            for half in range(2):
                nc.scalar.copy(e[:, half * N:(half + 1) * N], banks[u][half][:])
            return e

        def first_pick(u):
            first = keep.tile([P, N], F32, name="first", tag=max_tag[PACK + u], align_bytes=64)
            nc.vector.tensor_copy(first[:], es[u][:].indirect(l_pos1[:]))
            return first

        def add_closure(u, prod):
            res = keep.tile([P, N], F32, name="res", tag=("x6", "x7", "x0", "x3")[u], align_bytes=64)
            nc.vector.tensor_tensor(res[:], prod[:], clo[:, u, :], ALU.add)
            nc.sync.dma_start(out[u * P:(u + 1) * P, :], res[:])

        es = [scores(u) for u in range(OUT_TILES)]
        picked1 = first_pick(0)
        for u in range(OUT_TILES):
            prod = two.tile([P, N], F32, name="prod", tag="g", align_bytes=64)
            nc.vector.tensor_tensor(prod[:], es[u][:].indirect(l_pos2[:]), picked1[:], ALU.mult)
            if u + 1 < OUT_TILES:
                picked1 = first_pick(u + 1)
            add_closure(u, prod)
